import numpy as np
import ml_dtypes


def mxq(x, axis, fmt="e4m3"):
    dtype, down = {"e4m3": (ml_dtypes.float8_e4m3fn, 7), "e5m2": (ml_dtypes.float8_e5m2, 14)}[fmt]
    v = np.moveaxis(np.asarray(x, np.float32).astype(ml_dtypes.bfloat16).astype(np.float64), axis, -1)
    blocks = v.reshape(v.shape[:-1] + (-1, 32))
    amax = np.abs(blocks).max(-1, keepdims=True)
    byte = np.maximum(np.where(amax > 0, np.frexp(amax)[1] - 1 + 127, 0) - down, 1)
    scale = np.exp2(byte - 127.0)
    codes = (blocks / scale).astype(np.float32).astype(dtype).astype(np.float64)
    return np.moveaxis((codes * scale).reshape(v.shape), -1, axis)


WIDE = False


def mx_kscale(k):
    if not WIDE:
        return np.ones(k)
    levels = np.array([10, -10, 5, -5, 0])
    if k % 512:
        return np.exp2(np.random.permutation(np.resize(levels, k // 32))).repeat(32)
    a = np.empty((k // 512, 16))
    for p in range(k // 512):
        a[p, :8] = np.random.permutation(np.resize(levels, 8))
        for g in range(8):
            far = levels[np.abs(levels - a[p, g]) >= 10]
            a[p, g + 8] = far[np.random.randint(len(far))]
    return np.exp2(a.ravel()).repeat(32)


def f64(x):
    return np.asarray(x).astype(np.float64)


def striped(idx):
    return np.tile(idx.reshape(-1, 16).T, (8, 1)).astype(np.uint16)


def unstriped(offs):
    return offs[:16].T.reshape(-1).astype(np.int64)


K, T, D, S, V, N = 512, 1024, 4, 1024, 256, 256
P = 2 ** 7


def setup_inputs():
    n = np.random.standard_normal
    s = mx_kscale(K)[:, None]
    return {
        "xT": (n((K, T)) * s / np.sqrt(D)).astype(ml_dtypes.bfloat16).astype(np.float32),
        "w": (n((K, N)) / np.sqrt(K) / s).astype(np.float32),
        "gate": np.tile(np.random.uniform(0.5, 1.5, (D, 1, V)), (1, P, 1)).astype(ml_dtypes.bfloat16).astype(np.float32),
        "offs": striped(np.concatenate([np.random.permutation(T)[:V] for _ in range(D)])),
    }


def reference(xT, w, gate, offs):
    idx = unstriped(offs)
    x = sum(f64(gate)[d, :1] * f64(xT)[:, idx[d * V:(d + 1) * V]] for d in range(D))
    return mxq(f64(w), 0, "e4m3").T @ mxq(x, 0, "e4m3")

@@ -1,0 +1,167 @@
+from contextlib import ExitStack
+
+import concourse.mybir as mybir
+from concourse.masks import make_identity
+
+K, T, D, V, N = 512, 1024, 4, 256, 256
+P = 128
+PACK = 4
+F32 = mybir.dt.float32
+BF16 = mybir.dt.bfloat16
+U32 = mybir.dt.uint32
+U16 = mybir.dt.uint16
+I32 = mybir.dt.int32
+U8 = mybir.dt.uint8
+FP8X4 = mybir.dt.float8_e4m3fn_x4
+COPY = mybir.ActivationFunctionType.Copy
+MULT = mybir.AluOpType.mult
+
+WARM_UP = 20
+FLOPS = 2 * K * N * V
+CHUNKS = ((0, 512), (512, 768), (768, 1024))
+
+
+def tile_picked_bag_lin_none_sub_l_kernel(tc, xT, w, gate, offs, out):
+    nc = tc.nc
+    with ExitStack() as ctx:
+        held = ctx.enter_context(tc.tile_pool(name="held", bufs=1))
+        ring = ctx.enter_context(tc.tile_pool(name="ring", bufs=4))
+        fwd_pool = ctx.enter_context(tc.psum_pool(name="fwd", bufs=6))
+        sum_pool = ctx.enter_context(tc.psum_pool(name="sums", bufs=1))
+
+        offsets = held.tile([P, D * V // 16], U16, name="offsets")
+        ident = held.tile([P, P], F32, name="ident")
+        gate_rows = held.tile([P, P], F32, name="gate_rows")
+        gate_cols = held.tile([P, 2 * D], F32, name="gate_cols")
+        warm = held.tile([P, 2], F32, name="warm")
+        pairs = [held.tile([P, 2, T, 2], BF16, name=f"pair{u}") for u in range(2)]
+        w_raw = held.tile([P, PACK, N], F32, name="w_raw")
+
+        x_words = xT.bitcast(I32).rearrange("(p t) c -> p t c", t=PACK)
+
+        def load_pair(u, c0, c1):
+            nc.sync.dma_start(
+                out=pairs[u][:].rearrange("p t c h -> p t (c h)").bitcast(I32)[:, :, c0:c1],
+                in_=x_words[:, 2 * u : 2 * u + 2, c0:c1],
+            )
+
+        nc.vector.memset(gate_rows[:], 0.0)
+        nc.vector.memset(warm[:], 0.0)
+        nc.scalar.activation(warm[:, 1:2], warm[:, 0:1], COPY)
+        make_identity(nc, ident[:])
+
+        load_pair(0, *CHUNKS[0])
+        nc.sync.dma_start(offsets[:], offs)
+        for c in CHUNKS[1:]:
+            load_pair(0, *c)
+        gate_flat = gate.rearrange("d p (b v) -> (d p b) v", b=2)
+        nc.sync.dma_start(out=gate_rows[0 : 2 * D, :], in_=gate_flat[0 : 129 * (2 * D - 1) + 1 : 129, :])
+        for c in CHUNKS:
+            load_pair(1, *c)
+        nc.sync.dma_start(out=w_raw[:], in_=w.rearrange("(p t) n -> p t n", t=PACK))
+
+        idle = fwd_pool.tile([P, PACK, P], F32, name="fwd")
+        for j in range(WARM_UP):
+            nc.tensor.transpose(idle[:, j % PACK, :], ident[:], ident[:])
+
+        gate_ps = fwd_pool.tile([P, P], F32, name="fwd")
+        nc.tensor.transpose(gate_ps[:], gate_rows[:], ident[:])
+        nc.scalar.copy(gate_cols[:], gate_ps[:, 0 : 2 * D])
+
+        sums = [sum_pool.tile([P, PACK, P], F32, name=f"sum{b}") for b in range(2)]
+
+        units = [(u, d) for u in range(2) for d in range(D)]
+        last = len(units) - 1
+        turned = {}
+        prods = {}
+
+        def pick(i):
+            u, d = units[i]
+            if d == 0:
+                for c0, c1 in CHUNKS:
+                    if u == 0 or c0 > 0:
+                        nc.vector.tensor_copy(out=pairs[u][:, 1, c0:c1, 0], in_=pairs[u][:, 0, c0:c1, 1])
+                    else:
+                        nc.scalar.copy(pairs[u][:, 1, c0:c1, 0], pairs[u][:, 0, c0:c1, 1])
+            window = pairs[u][:, 1, :, :].rearrange("p c h -> p (c h)").bitcast(U32)
+            picked = ring.tile([P, V], U32, name="picked")
+            nc.vector.tensor_copy(picked[:], window.indirect(offsets[:, d * V // 16 : (d + 1) * V // 16]))
+            if i < last - 1:
+                bank = fwd_pool.tile([P, 2, P], F32, name="fwd")
+                views = [bank[:, b, :] for b in range(2)]
+            else:
+                views = [fwd_pool.tile([P, P], F32, name="fwd")[:] for b in range(2)]
+            for b in range(2):
+                nc.tensor.transpose(views[b], picked[:, b * P : (b + 1) * P].bitcast(F32), ident[:])
+                turned[i, b] = views[b]
+
+        def weigh(i):
+            u, d = units[i]
+            for b in range(2):
+                prod = ring.tile([P, 2, P], F32, name="prod", bufs=8)
+                src = turned[i, b].bitcast(BF16).rearrange("v (p e) -> v e p", e=2)
+                g = gate_cols[:, 2 * d + b : 2 * d + b + 1]
+                if i >= last - 1 and b == 1:
+                    nc.vector.tensor_scalar(prod[:], src, g, None, MULT)
+                else:
+                    nc.scalar.activation(prod[:], src, COPY, scale=g)
+                prods[i, b] = prod
+
+        def add_up(i):
+            u, d = units[i]
+            for b in range(2):
+                for e in range(2):
+                    nc.tensor.matmul(
+                        sums[b][:, 2 * u + e, :],
+                        prods[i, b][:, e, :],
+                        ident[:],
+                        start=(i == 0 and e == 0),
+                        stop=(i == last and e == 1),
+                        is_transpose=True,
+                    )
+
+        for step in range(len(units) + 2):
+            if step <= last:
+                pick(step)
+            if 0 <= step - 1 <= last:
+                weigh(step - 1)
+            if 0 <= step - 2 <= last:
+                add_up(step - 2)
+
+        w_grouped = held.tile([P, N, PACK], BF16, name="w_grouped", align_bytes=64)
+        w_codes = held.tile([P, N], U32, name="w_codes", align_bytes=64)
+        w_scales = held.tile([P, N], U8, name="w_scales", align_bytes=64)
+        for h in range(2):
+            cols = slice(h * P, (h + 1) * P)
+            nc.vector.tensor_copy(out=w_grouped[:, cols, :], in_=w_raw[:, :, cols].rearrange("p t n -> p n t"))
+        nc.vector.quantize_mx(
+            out=w_codes[:].bitcast(FP8X4), scales=w_scales[:], in_=w_grouped[:].rearrange("p n t -> p (n t)")
+        )
+
+        x_grouped = held.tile([P, V, PACK], BF16, name="x_grouped", align_bytes=64)
+        nc.scalar.copy(x_grouped[:, 0:P, :], sums[0][:].rearrange("p t v -> p v t"))
+        nc.vector.tensor_copy(out=x_grouped[:, P:V, :], in_=sums[1][:].rearrange("p t v -> p v t"))
+        x_codes = held.tile([P, V], U32, name="x_codes", align_bytes=64)
+        x_scales = held.tile([P, V], U8, name="x_scales", align_bytes=64)
+        nc.vector.quantize_mx(
+            out=x_codes[:].bitcast(FP8X4), scales=x_scales[:], in_=x_grouped[:].rearrange("p v t -> p (v t)")
+        )
+
+        for h in range(2):
+            acc = fwd_pool.tile([P, V], F32, name="fwd")
+            nc.tensor.matmul_mx(
+                out=acc[:],
+                lhsT=w_codes[:, h * P : (h + 1) * P].bitcast(FP8X4),
+                lhsT_scale=w_scales[:, h * P : (h + 1) * P],
+                rhs=x_codes[:].bitcast(FP8X4),
+                rhs_scale=x_scales[:],
+                start=True,
+                stop=True,
+            )
+            result = held.tile([P, V], F32, name=f"result{h}")
+            if h == 0:
+                nc.vector.tensor_copy(out=result[:], in_=acc[:])
+                nc.sync.dma_start(out=out[h * P : (h + 1) * P, :], in_=result[:])
+            else:
+                nc.scalar.copy(result[:], acc[:])
+                nc.scalar.dma_start(out=out[h * P : (h + 1) * P, :], in_=result[:])

@@ -15,8 +15,9 @@ U8 = mybir.dt.uint8
 FP8X4 = mybir.dt.float8_e4m3fn_x4
 COPY = mybir.ActivationFunctionType.Copy
 MULT = mybir.AluOpType.mult
+ADD = mybir.AluOpType.add
 
-WARM_UP = 20
+FUSED = (1, 5, 6, 7)
 FLOPS = 2 * K * N * V
 CHUNKS = ((0, 512), (512, 768), (768, 1024))
 
@@ -26,7 +27,7 @@ def tile_picked_bag_lin_none_sub_l_kernel(tc, xT, w, gate, offs, out):
     with ExitStack() as ctx:
         held = ctx.enter_context(tc.tile_pool(name="held", bufs=1))
         ring = ctx.enter_context(tc.tile_pool(name="ring", bufs=4))
-        fwd_pool = ctx.enter_context(tc.psum_pool(name="fwd", bufs=6))
+        fwd_pool = ctx.enter_context(tc.psum_pool(name="fwd", bufs=5))
         sum_pool = ctx.enter_context(tc.psum_pool(name="sums", bufs=1))
 
         offsets = held.tile([P, D * V // 16], U16, name="offsets")
@@ -60,87 +61,101 @@ def tile_picked_bag_lin_none_sub_l_kernel(tc, xT, w, gate, offs, out):
             load_pair(1, *c)
         nc.sync.dma_start(out=w_raw[:], in_=w.rearrange("(p t) n -> p t n", t=PACK))
 
-        idle = fwd_pool.tile([P, PACK, P], F32, name="fwd")
-        for j in range(WARM_UP):
-            nc.tensor.transpose(idle[:, j % PACK, :], ident[:], ident[:])
-
         gate_ps = fwd_pool.tile([P, P], F32, name="fwd")
         nc.tensor.transpose(gate_ps[:], gate_rows[:], ident[:])
         nc.scalar.copy(gate_cols[:], gate_ps[:, 0 : 2 * D])
 
-        sums = [sum_pool.tile([P, PACK, P], F32, name=f"sum{b}") for b in range(2)]
+        sum_low = sum_pool.tile([P, 2, 2, P], F32, name="sum_low")
+        sum_high = [sum_pool.tile([P, P], F32, name=f"sum_high{b}") for b in range(2)]
+        x_grouped = held.tile([P, V, PACK], BF16, name="x_grouped", align_bytes=64)
+        w_grouped = held.tile([P, N, PACK], BF16, name="w_grouped", align_bytes=64)
+        w_codes = held.tile([P, N], U32, name="w_codes", align_bytes=64)
+        w_scales = held.tile([P, N], U8, name="w_scales", align_bytes=64)
 
         units = [(u, d) for u in range(2) for d in range(D)]
         last = len(units) - 1
+        fused = FUSED
         turned = {}
-        prods = {}
+        terms = {}
 
         def pick(i):
             u, d = units[i]
             if d == 0:
                 for c0, c1 in CHUNKS:
-                    if u == 0 or c0 > 0:
+                    if u == 0:
                         nc.vector.tensor_copy(out=pairs[u][:, 1, c0:c1, 0], in_=pairs[u][:, 0, c0:c1, 1])
                     else:
                         nc.scalar.copy(pairs[u][:, 1, c0:c1, 0], pairs[u][:, 0, c0:c1, 1])
             window = pairs[u][:, 1, :, :].rearrange("p c h -> p (c h)").bitcast(U32)
             picked = ring.tile([P, V], U32, name="picked")
             nc.vector.tensor_copy(picked[:], window.indirect(offsets[:, d * V // 16 : (d + 1) * V // 16]))
-            if i < last - 1:
-                bank = fwd_pool.tile([P, 2, P], F32, name="fwd")
-                views = [bank[:, b, :] for b in range(2)]
-            else:
-                views = [fwd_pool.tile([P, P], F32, name="fwd")[:] for b in range(2)]
+            bank = fwd_pool.tile([P, 2, P], F32, name="fwd")
             for b in range(2):
-                nc.tensor.transpose(views[b], picked[:, b * P : (b + 1) * P].bitcast(F32), ident[:])
-                turned[i, b] = views[b]
+                nc.tensor.transpose(bank[:, b, :], picked[:, b * P : (b + 1) * P].bitcast(F32), ident[:])
+            turned[i] = bank
 
         def weigh(i):
             u, d = units[i]
             for b in range(2):
-                prod = ring.tile([P, 2, P], F32, name="prod", bufs=8)
-                src = turned[i, b].bitcast(BF16).rearrange("v (p e) -> v e p", e=2)
-                g = gate_cols[:, 2 * d + b : 2 * d + b + 1]
-                if i >= last - 1 and b == 1:
-                    nc.vector.tensor_scalar(prod[:], src, g, None, MULT)
+                src = turned[i][:, b, :].bitcast(BF16)
+                if i == last:
+                    term = ring.tile([P, 2 * P], BF16, name="rounded")
                 else:
-                    nc.scalar.activation(prod[:], src, COPY, scale=g)
-                prods[i, b] = prod
+                    term = ring.tile([P, 2 * P], F32, name="term", bufs=14)
+                dst = term[:]
+                if u == 0:
+                    src = src.rearrange("v (p e) -> v e p", e=2)
+                    dst = dst.rearrange("v (e p) -> v e p", e=2)
+                g = gate_cols[:, 2 * d + b : 2 * d + b + 1]
+                if i in fused:
+                    prev = terms[i - 1, b][:]
+                    if u == 0:
+                        prev = prev.rearrange("v (e p) -> v e p", e=2)
+                    nc.vector.scalar_tensor_tensor(dst, src, g, prev, MULT, ADD)
+                else:
+                    nc.scalar.activation(dst, src, COPY, scale=g)
+                terms[i, b] = term
+
+        low_terms = [i for i in range(D) if i + 1 not in fused or i == D - 1]
 
         def add_up(i):
-            u, d = units[i]
+            if i not in low_terms:
+                return
             for b in range(2):
                 for e in range(2):
                     nc.tensor.matmul(
-                        sums[b][:, 2 * u + e, :],
-                        prods[i, b][:, e, :],
+                        sum_low[:, b, e, :],
+                        terms[i, b][:, e * P : (e + 1) * P],
                         ident[:],
-                        start=(i == 0 and e == 0),
-                        stop=(i == last and e == 1),
+                        start=(i == low_terms[0] and b == 0 and e == 0),
+                        stop=(i == low_terms[-1] and b == 1 and e == 1),
                         is_transpose=True,
                     )
 
-        for step in range(len(units) + 2):
+        for step in range(len(units) + 1):
             if step <= last:
                 pick(step)
             if 0 <= step - 1 <= last:
                 weigh(step - 1)
-            if 0 <= step - 2 <= last:
-                add_up(step - 2)
+            add_up(step - 2)
 
-        w_grouped = held.tile([P, N, PACK], BF16, name="w_grouped", align_bytes=64)
-        w_codes = held.tile([P, N], U32, name="w_codes", align_bytes=64)
-        w_scales = held.tile([P, N], U8, name="w_scales", align_bytes=64)
+        nc.scalar.copy(
+            x_grouped[:, :, 0:2].rearrange("p (b v) e -> p b v e", b=2), sum_low[:].rearrange("p b e v -> p b v e")
+        )
         for h in range(2):
             cols = slice(h * P, (h + 1) * P)
-            nc.vector.tensor_copy(out=w_grouped[:, cols, :], in_=w_raw[:, :, cols].rearrange("p t n -> p n t"))
+            nc.scalar.copy(w_grouped[:, cols, :], w_raw[:, :, cols].rearrange("p t n -> p n t"))
         nc.vector.quantize_mx(
             out=w_codes[:].bitcast(FP8X4), scales=w_scales[:], in_=w_grouped[:].rearrange("p n t -> p (n t)")
         )
 
-        x_grouped = held.tile([P, V, PACK], BF16, name="x_grouped", align_bytes=64)
-        nc.scalar.copy(x_grouped[:, 0:P, :], sums[0][:].rearrange("p t v -> p v t"))
-        nc.vector.tensor_copy(out=x_grouped[:, P:V, :], in_=sums[1][:].rearrange("p t v -> p v t"))
+        for b in range(2):
+            nc.tensor.transpose(sum_high[b][:], terms[last, b][:].bitcast(F32), ident[:])
+            src = sum_high[b][:].bitcast(BF16).rearrange("p (v e) -> p v e", e=2)
+            if b == 0:
+                nc.scalar.copy(x_grouped[:, 0:P, 2:4], src)
+            else:
+                nc.vector.tensor_copy(out=x_grouped[:, P:V, 2:4], in_=src)
         x_codes = held.tile([P, V], U32, name="x_codes", align_bytes=64)
         x_scales = held.tile([P, V], U8, name="x_scales", align_bytes=64)
         nc.vector.quantize_mx(

@@ -17,7 +17,7 @@ COPY = mybir.ActivationFunctionType.Copy
 MULT = mybir.AluOpType.mult
 ADD = mybir.AluOpType.add
 
-FUSED = (1, 5, 6, 7)
+FUSED = (6, 7)
 FLOPS = 2 * K * N * V
 CHUNKS = ((0, 512), (512, 768), (768, 1024))
 
@@ -27,7 +27,7 @@ def tile_picked_bag_lin_none_sub_l_kernel(tc, xT, w, gate, offs, out):
     with ExitStack() as ctx:
         held = ctx.enter_context(tc.tile_pool(name="held", bufs=1))
         ring = ctx.enter_context(tc.tile_pool(name="ring", bufs=4))
-        fwd_pool = ctx.enter_context(tc.psum_pool(name="fwd", bufs=5))
+        fwd_pool = ctx.enter_context(tc.psum_pool(name="fwd", bufs=6))
         sum_pool = ctx.enter_context(tc.psum_pool(name="sums", bufs=1))
 
         offsets = held.tile([P, D * V // 16], U16, name="offsets")
@@ -40,10 +40,10 @@ def tile_picked_bag_lin_none_sub_l_kernel(tc, xT, w, gate, offs, out):
 
         x_words = xT.bitcast(I32).rearrange("(p t) c -> p t c", t=PACK)
 
-        def load_pair(u, c0, c1):
+        def load(u, rows, c0, c1):
             nc.sync.dma_start(
-                out=pairs[u][:].rearrange("p t c h -> p t (c h)").bitcast(I32)[:, :, c0:c1],
-                in_=x_words[:, 2 * u : 2 * u + 2, c0:c1],
+                out=pairs[u][:].rearrange("p t c h -> p t (c h)").bitcast(I32)[:, rows, c0:c1],
+                in_=x_words[:, 2 * u : 2 * u + 2, :][:, rows, c0:c1],
             )
 
         nc.vector.memset(gate_rows[:], 0.0)
@@ -51,25 +51,26 @@ def tile_picked_bag_lin_none_sub_l_kernel(tc, xT, w, gate, offs, out):
         nc.scalar.activation(warm[:, 1:2], warm[:, 0:1], COPY)
         make_identity(nc, ident[:])
 
-        load_pair(0, *CHUNKS[0])
+        load(0, slice(0, 1), 0, T)
         nc.sync.dma_start(offsets[:], offs)
-        for c in CHUNKS[1:]:
-            load_pair(0, *c)
+        for c0, c1 in CHUNKS:
+            load(0, slice(1, 2), c0, c1)
         gate_flat = gate.rearrange("d p (b v) -> (d p b) v", b=2)
         nc.sync.dma_start(out=gate_rows[0 : 2 * D, :], in_=gate_flat[0 : 129 * (2 * D - 1) + 1 : 129, :])
-        for c in CHUNKS:
-            load_pair(1, *c)
+        for c0, c1 in CHUNKS[:-1]:
+            load(1, slice(0, 2), c0, c1)
+        c0, c1 = CHUNKS[-1]
+        low_end = held.tile([P, c1 - c0, 2], BF16, name="low_end", tag="before_first_add")
+        nc.sync.dma_start(out=low_end[:].rearrange("p c h -> p (c h)").bitcast(I32), in_=x_words[:, 2, c0:c1])
+        load(1, slice(1, 2), c0, c1)
         nc.sync.dma_start(out=w_raw[:], in_=w.rearrange("(p t) n -> p t n", t=PACK))
 
         gate_ps = fwd_pool.tile([P, P], F32, name="fwd")
         nc.tensor.transpose(gate_ps[:], gate_rows[:], ident[:])
         nc.scalar.copy(gate_cols[:], gate_ps[:, 0 : 2 * D])
 
-        sum_low = sum_pool.tile([P, 2, 2, P], F32, name="sum_low")
-        sum_high = [sum_pool.tile([P, P], F32, name=f"sum_high{b}") for b in range(2)]
+        sums = [sum_pool.tile([P, PACK, P], F32, name=f"sum{b}") for b in range(2)]
         x_grouped = held.tile([P, V, PACK], BF16, name="x_grouped", align_bytes=64)
-        w_grouped = held.tile([P, N, PACK], BF16, name="w_grouped", align_bytes=64)
-        w_codes = held.tile([P, N], U32, name="w_codes", align_bytes=64)
         w_scales = held.tile([P, N], U8, name="w_scales", align_bytes=64)
 
         units = [(u, d) for u in range(2) for d in range(D)]
@@ -77,106 +78,130 @@ def tile_picked_bag_lin_none_sub_l_kernel(tc, xT, w, gate, offs, out):
         fused = FUSED
         turned = {}
         terms = {}
+        wide = {}
 
         def pick(i):
             u, d = units[i]
             if d == 0:
                 for c0, c1 in CHUNKS:
                     if u == 0:
-                        nc.vector.tensor_copy(out=pairs[u][:, 1, c0:c1, 0], in_=pairs[u][:, 0, c0:c1, 1])
-                    else:
+                        mid = (c0 + c1) // 2
+                        nc.vector.tensor_copy(out=pairs[u][:, 1, c0:mid, 0], in_=pairs[u][:, 0, c0:mid, 1])
+                        nc.scalar.copy(pairs[u][:, 1, mid:c1, 0], pairs[u][:, 0, mid:c1, 1])
+                    elif c0 == 0:
                         nc.scalar.copy(pairs[u][:, 1, c0:c1, 0], pairs[u][:, 0, c0:c1, 1])
+                    else:
+                        low = low_end[:, :, 1] if c1 == T else pairs[u][:, 0, c0:c1, 1]
+                        nc.gpsimd.tensor_scalar(pairs[u][:, 1, c0:c1, 0], low, 1.0, 0.0, MULT, ADD)
             window = pairs[u][:, 1, :, :].rearrange("p c h -> p (c h)").bitcast(U32)
-            picked = ring.tile([P, V], U32, name="picked")
-            nc.vector.tensor_copy(picked[:], window.indirect(offsets[:, d * V // 16 : (d + 1) * V // 16]))
-            bank = fwd_pool.tile([P, 2, P], F32, name="fwd")
+            if i == 5:
+                picked = held.tile([P, V], U32, name="picked_late", tag="before_w_grouped", align_bytes=64)
+            else:
+                picked = ring.tile([P, V], U32, name="picked")
+            if i == 0:
+                for b in range(2):
+                    nc.vector.tensor_copy(
+                        picked[:, b * P : (b + 1) * P], window.indirect(offsets[:, b * P // 16 : (b + 1) * P // 16])
+                    )
+                views = [fwd_pool.tile([P, P], F32, name="fwd")[:] for b in range(2)]
+            else:
+                nc.vector.tensor_copy(picked[:], window.indirect(offsets[:, d * V // 16 : (d + 1) * V // 16]))
+                bank = fwd_pool.tile([P, 2, P], F32, name="fwd")
+                views = [bank[:, b, :] for b in range(2)]
             for b in range(2):
-                nc.tensor.transpose(bank[:, b, :], picked[:, b * P : (b + 1) * P].bitcast(F32), ident[:])
-            turned[i] = bank
+                nc.tensor.transpose(views[b], picked[:, b * P : (b + 1) * P].bitcast(F32), ident[:])
+                turned[i, b] = views[b]
 
         def weigh(i):
             u, d = units[i]
+            if u == 0:
+                wide[i] = ring.tile([P, 2, 2 * P], F32, name="wide")
             for b in range(2):
-                src = turned[i][:, b, :].bitcast(BF16)
-                if i == last:
-                    term = ring.tile([P, 2 * P], BF16, name="rounded")
-                else:
-                    term = ring.tile([P, 2 * P], F32, name="term", bufs=14)
-                dst = term[:]
+                src = turned[i, b].bitcast(BF16)
                 if u == 0:
-                    src = src.rearrange("v (p e) -> v e p", e=2)
-                    dst = dst.rearrange("v (e p) -> v e p", e=2)
+                    term = wide[i][:, b, :]
+                elif i == last - 1 and b == 1:
+                    term = held.tile([P, 2 * P], F32, name="term_late", tag="before_w_codes", align_bytes=64)
+                else:
+                    term = ring.tile([P, 2 * P], F32, name="term", bufs=7)
+                dst = term[:]
+                src = src.rearrange("v (p e) -> v e p", e=2)
+                dst = dst.rearrange("v (e p) -> v e p", e=2)
                 g = gate_cols[:, 2 * d + b : 2 * d + b + 1]
                 if i in fused:
-                    prev = terms[i - 1, b][:]
-                    if u == 0:
-                        prev = prev.rearrange("v (e p) -> v e p", e=2)
+                    prev = terms[i - 1, b][:].rearrange("v (e p) -> v e p", e=2)
                     nc.vector.scalar_tensor_tensor(dst, src, g, prev, MULT, ADD)
                 else:
                     nc.scalar.activation(dst, src, COPY, scale=g)
                 terms[i, b] = term
 
-        low_terms = [i for i in range(D) if i + 1 not in fused or i == D - 1]
+        def add_two(i):
+            both = held.tile([P, 2, 2 * P], F32, name="both", tag="before_first_add" if i == 1 else "both")
+            nc.gpsimd.tensor_tensor(both[:], wide[i - 1][:], wide[i][:], ADD)
+            for b in range(2):
+                terms[i, b] = both[:, b, :]
 
         def add_up(i):
-            if i not in low_terms:
-                return
+            u = units[i][0]
             for b in range(2):
                 for e in range(2):
                     nc.tensor.matmul(
-                        sum_low[:, b, e, :],
+                        sums[b][:, 2 * u + e, :],
                         terms[i, b][:, e * P : (e + 1) * P],
                         ident[:],
-                        start=(i == low_terms[0] and b == 0 and e == 0),
-                        stop=(i == low_terms[-1] and b == 1 and e == 1),
+                        start=(i == 1 and e == 0),
+                        stop=(i == last and e == 1),
                         is_transpose=True,
                     )
 
         for step in range(len(units) + 1):
             if step <= last:
                 pick(step)
-            if 0 <= step - 1 <= last:
+            if step >= 1:
                 weigh(step - 1)
-            add_up(step - 2)
+            if step - 3 in (1, 3):
+                add_two(step - 3)
+        for i in (1, 4, 3, 7):
+            add_up(i)
 
-        nc.scalar.copy(
-            x_grouped[:, :, 0:2].rearrange("p (b v) e -> p b v e", b=2), sum_low[:].rearrange("p b e v -> p b v e")
-        )
-        for h in range(2):
-            cols = slice(h * P, (h + 1) * P)
-            nc.scalar.copy(w_grouped[:, cols, :], w_raw[:, :, cols].rearrange("p t n -> p n t"))
+        w_grouped = held.tile([P, N, PACK], BF16, name="w_grouped", tag="before_w_grouped", align_bytes=64)
+        w_codes = held.tile([P, N], U32, name="w_codes", tag="before_w_codes", align_bytes=64)
+        nc.scalar.copy(w_grouped[:], w_raw[:].rearrange("p t n -> p n t"))
         nc.vector.quantize_mx(
             out=w_codes[:].bitcast(FP8X4), scales=w_scales[:], in_=w_grouped[:].rearrange("p n t -> p (n t)")
         )
 
-        for b in range(2):
-            nc.tensor.transpose(sum_high[b][:], terms[last, b][:].bitcast(F32), ident[:])
-            src = sum_high[b][:].bitcast(BF16).rearrange("p (v e) -> p v e", e=2)
-            if b == 0:
-                nc.scalar.copy(x_grouped[:, 0:P, 2:4], src)
-            else:
-                nc.vector.tensor_copy(out=x_grouped[:, P:V, 2:4], in_=src)
         x_codes = held.tile([P, V], U32, name="x_codes", align_bytes=64)
         x_scales = held.tile([P, V], U8, name="x_scales", align_bytes=64)
-        nc.vector.quantize_mx(
-            out=x_codes[:].bitcast(FP8X4), scales=x_scales[:], in_=x_grouped[:].rearrange("p v t -> p (v t)")
-        )
-
-        for h in range(2):
-            acc = fwd_pool.tile([P, V], F32, name="fwd")
-            nc.tensor.matmul_mx(
-                out=acc[:],
-                lhsT=w_codes[:, h * P : (h + 1) * P].bitcast(FP8X4),
-                lhsT_scale=w_scales[:, h * P : (h + 1) * P],
-                rhs=x_codes[:].bitcast(FP8X4),
-                rhs_scale=x_scales[:],
-                start=True,
-                stop=True,
-            )
-            result = held.tile([P, V], F32, name=f"result{h}")
-            if h == 0:
-                nc.vector.tensor_copy(out=result[:], in_=acc[:])
-                nc.sync.dma_start(out=out[h * P : (h + 1) * P, :], in_=result[:])
+        results = [held.tile([P, V], F32, name=f"result{h}") for h in range(2)]
+        for b in range(2):
+            bags = slice(b * P, (b + 1) * P)
+            src = sums[b][:].rearrange("p t v -> p v t")
+            if b == 0:
+                nc.vector.tensor_copy(out=x_grouped[:, bags, :], in_=src)
             else:
-                nc.scalar.copy(result[:], acc[:])
-                nc.scalar.dma_start(out=out[h * P : (h + 1) * P, :], in_=result[:])
+                nc.scalar.copy(x_grouped[:, bags, :], src)
+        for b in range(2):
+            bags = slice(b * P, (b + 1) * P)
+            nc.vector.quantize_mx(
+                out=x_codes[:, bags].bitcast(FP8X4),
+                scales=x_scales[:, bags],
+                in_=x_grouped[:, bags, :].rearrange("p v t -> p (v t)"),
+            )
+            for h in range(2):
+                acc = fwd_pool.tile([P, P], F32, name="fwd")
+                nc.tensor.matmul_mx(
+                    out=acc[:],
+                    lhsT=w_codes[:, h * P : (h + 1) * P].bitcast(FP8X4),
+                    lhsT_scale=w_scales[:, h * P : (h + 1) * P],
+                    rhs=x_codes[:, bags].bitcast(FP8X4),
+                    rhs_scale=x_scales[:, bags],
+                    start=True,
+                    stop=True,
+                )
+                if h == 0 and b == 1:
+                    nc.vector.tensor_copy(out=results[h][:, bags], in_=acc[:])
+                else:
+                    nc.scalar.copy(results[h][:, bags], acc[:])
+        nc.sync.dma_start(out=out[0:P, :], in_=results[0][:])
+        nc.scalar.dma_start(out=out[P:N, :], in_=results[1][:])

@@ -166,42 +166,46 @@ def tile_picked_bag_lin_none_sub_l_kernel(tc, xT, w, gate, offs, out):
 
         w_grouped = held.tile([P, N, PACK], BF16, name="w_grouped", tag="before_w_grouped", align_bytes=64)
         w_codes = held.tile([P, N], U32, name="w_codes", tag="before_w_codes", align_bytes=64)
-        nc.scalar.copy(w_grouped[:], w_raw[:].rearrange("p t n -> p n t"))
-        nc.vector.quantize_mx(
-            out=w_codes[:].bitcast(FP8X4), scales=w_scales[:], in_=w_grouped[:].rearrange("p n t -> p (n t)")
-        )
+        halves = [slice(0, P), slice(P, 2 * P)]
+        for cols in halves:
+            nc.scalar.copy(w_grouped[:, cols, :], w_raw[:, :, cols].rearrange("p t n -> p n t"))
+
+        def quantize(codes, scales, grouped, cols):
+            nc.vector.quantize_mx(
+                out=codes[:, cols].bitcast(FP8X4),
+                scales=scales[:, cols],
+                in_=grouped[:, cols, :].rearrange("p c t -> p (c t)"),
+            )
 
         x_codes = held.tile([P, V], U32, name="x_codes", align_bytes=64)
         x_scales = held.tile([P, V], U8, name="x_scales", align_bytes=64)
-        results = [held.tile([P, V], F32, name=f"result{h}") for h in range(2)]
-        for b in range(2):
-            bags = slice(b * P, (b + 1) * P)
-            src = sums[b][:].rearrange("p t v -> p v t")
-            if b == 0:
-                nc.vector.tensor_copy(out=x_grouped[:, bags, :], in_=src)
-            else:
-                nc.scalar.copy(x_grouped[:, bags, :], src)
-        for b in range(2):
-            bags = slice(b * P, (b + 1) * P)
-            nc.vector.quantize_mx(
-                out=x_codes[:, bags].bitcast(FP8X4),
-                scales=x_scales[:, bags],
-                in_=x_grouped[:, bags, :].rearrange("p v t -> p (v t)"),
-            )
-            for h in range(2):
+        quantize(w_codes, w_scales, w_grouped, halves[0])
+        nc.vector.tensor_copy(out=x_grouped[:, halves[0], :], in_=sums[0][:].rearrange("p t v -> p v t"))
+        nc.scalar.copy(x_grouped[:, halves[1], :], sums[1][:].rearrange("p t v -> p v t"))
+        quantize(w_codes, w_scales, w_grouped, halves[1])
+
+        out_rows = out.rearrange("(h m) v -> m h v", h=2)
+        for b, bags in enumerate(halves):
+            quantize(x_codes, x_scales, x_grouped, bags)
+            result = held.tile([P, 2, P], F32, name=f"result{b}")
+            for h, cols in enumerate(halves):
                 acc = fwd_pool.tile([P, P], F32, name="fwd")
                 nc.tensor.matmul_mx(
                     out=acc[:],
-                    lhsT=w_codes[:, h * P : (h + 1) * P].bitcast(FP8X4),
-                    lhsT_scale=w_scales[:, h * P : (h + 1) * P],
+                    lhsT=w_codes[:, cols].bitcast(FP8X4),
+                    lhsT_scale=w_scales[:, cols],
                     rhs=x_codes[:, bags].bitcast(FP8X4),
                     rhs_scale=x_scales[:, bags],
                     start=True,
                     stop=True,
                 )
-                if h == 0 and b == 1:
-                    nc.vector.tensor_copy(out=results[h][:, bags], in_=acc[:])
+                if b == 0:
+                    nc.scalar.copy(result[:, h, :], acc[:])
+                elif h == 0:
+                    nc.vector.tensor_copy(out=result[:, h, :], in_=acc[:])
+                    nc.sync.dma_start(out=out_rows[:, h, bags], in_=result[:, h, :])
                 else:
-                    nc.scalar.copy(results[h][:, bags], acc[:])
-        nc.sync.dma_start(out=out[0:P, :], in_=results[0][:])
-        nc.scalar.dma_start(out=out[P:N, :], in_=results[1][:])
+                    nc.scalar.copy(result[:, h, :], acc[:])
+                    nc.scalar.dma_start(out=out_rows[:, h, bags], in_=result[:, h, :])
+            if b == 0:
+                nc.sync.dma_start(out=out_rows[:, :, bags], in_=result[:])

from contextlib import ExitStack

import concourse.mybir as mybir
from concourse.masks import make_identity

K, T, D, V, N = 512, 1024, 4, 256, 256
P = 128
PACK = 4
F32 = mybir.dt.float32
BF16 = mybir.dt.bfloat16
U32 = mybir.dt.uint32
U16 = mybir.dt.uint16
I32 = mybir.dt.int32
U8 = mybir.dt.uint8
FP8X4 = mybir.dt.float8_e4m3fn_x4
COPY = mybir.ActivationFunctionType.Copy
MULT = mybir.AluOpType.mult
ADD = mybir.AluOpType.add

FUSED = (6, 7)
FLOPS = 2 * K * N * V
CHUNKS = ((0, 512), (512, 768), (768, 1024))


def tile_picked_bag_lin_none_sub_l_kernel(tc, xT, w, gate, offs, out):
    nc = tc.nc
    with ExitStack() as ctx:
        held = ctx.enter_context(tc.tile_pool(name="held", bufs=1))
        ring = ctx.enter_context(tc.tile_pool(name="ring", bufs=4))
        fwd_pool = ctx.enter_context(tc.psum_pool(name="fwd", bufs=6))
        sum_pool = ctx.enter_context(tc.psum_pool(name="sums", bufs=1))

        offsets = held.tile([P, D * V // 16], U16, name="offsets")
        ident = held.tile([P, P], F32, name="ident")
        gate_rows = held.tile([P, P], F32, name="gate_rows")
        gate_cols = held.tile([P, 2 * D], F32, name="gate_cols")
        warm = held.tile([P, 2], F32, name="warm")
        pairs = [held.tile([P, 2, T, 2], BF16, name=f"pair{u}") for u in range(2)]
        w_raw = held.tile([P, PACK, N], F32, name="w_raw")

        x_words = xT.bitcast(I32).rearrange("(p t) c -> p t c", t=PACK)

        def load(u, rows, c0, c1):
            nc.sync.dma_start(
                out=pairs[u][:].rearrange("p t c h -> p t (c h)").bitcast(I32)[:, rows, c0:c1],
                in_=x_words[:, 2 * u : 2 * u + 2, :][:, rows, c0:c1],
            )

        nc.vector.memset(gate_rows[:], 0.0)
        nc.vector.memset(warm[:], 0.0)
        nc.scalar.activation(warm[:, 1:2], warm[:, 0:1], COPY)
        make_identity(nc, ident[:])

        load(0, slice(0, 1), 0, T)
        nc.sync.dma_start(offsets[:], offs)
        for c0, c1 in CHUNKS:
            load(0, slice(1, 2), c0, c1)
        gate_flat = gate.rearrange("d p (b v) -> (d p b) v", b=2)
        nc.sync.dma_start(out=gate_rows[0 : 2 * D, :], in_=gate_flat[0 : 129 * (2 * D - 1) + 1 : 129, :])
        for c0, c1 in CHUNKS[:-1]:
            load(1, slice(0, 2), c0, c1)
        c0, c1 = CHUNKS[-1]
        low_end = held.tile([P, c1 - c0, 2], BF16, name="low_end", tag="before_first_add")
        nc.sync.dma_start(out=low_end[:].rearrange("p c h -> p (c h)").bitcast(I32), in_=x_words[:, 2, c0:c1])
        load(1, slice(1, 2), c0, c1)
        nc.sync.dma_start(out=w_raw[:], in_=w.rearrange("(p t) n -> p t n", t=PACK))

        gate_ps = fwd_pool.tile([P, P], F32, name="fwd")
        nc.tensor.transpose(gate_ps[:], gate_rows[:], ident[:])
        nc.scalar.copy(gate_cols[:], gate_ps[:, 0 : 2 * D])

        sums = [sum_pool.tile([P, PACK, P], F32, name=f"sum{b}") for b in range(2)]
        x_grouped = held.tile([P, V, PACK], BF16, name="x_grouped", align_bytes=64)
        w_scales = held.tile([P, N], U8, name="w_scales", align_bytes=64)

        units = [(u, d) for u in range(2) for d in range(D)]
        last = len(units) - 1
        fused = FUSED
        turned = {}
        terms = {}
        wide = {}

        def pick(i):
            u, d = units[i]
            if d == 0:
                for c0, c1 in CHUNKS:
                    if u == 0:
                        mid = (c0 + c1) // 2
                        nc.vector.tensor_copy(out=pairs[u][:, 1, c0:mid, 0], in_=pairs[u][:, 0, c0:mid, 1])
                        nc.scalar.copy(pairs[u][:, 1, mid:c1, 0], pairs[u][:, 0, mid:c1, 1])
                    elif c0 == 0:
                        nc.scalar.copy(pairs[u][:, 1, c0:c1, 0], pairs[u][:, 0, c0:c1, 1])
                    else:
                        low = low_end[:, :, 1] if c1 == T else pairs[u][:, 0, c0:c1, 1]
                        nc.gpsimd.tensor_scalar(pairs[u][:, 1, c0:c1, 0], low, 1.0, 0.0, MULT, ADD)
            window = pairs[u][:, 1, :, :].rearrange("p c h -> p (c h)").bitcast(U32)
            if i == 5:
                picked = held.tile([P, V], U32, name="picked_late", tag="before_w_grouped", align_bytes=64)
            else:
                picked = ring.tile([P, V], U32, name="picked")
            if i == 0:
                for b in range(2):
                    nc.vector.tensor_copy(
                        picked[:, b * P : (b + 1) * P], window.indirect(offsets[:, b * P // 16 : (b + 1) * P // 16])
                    )
                views = [fwd_pool.tile([P, P], F32, name="fwd")[:] for b in range(2)]
            else:
                nc.vector.tensor_copy(picked[:], window.indirect(offsets[:, d * V // 16 : (d + 1) * V // 16]))
                bank = fwd_pool.tile([P, 2, P], F32, name="fwd")
                views = [bank[:, b, :] for b in range(2)]
            for b in range(2):
                nc.tensor.transpose(views[b], picked[:, b * P : (b + 1) * P].bitcast(F32), ident[:])
                turned[i, b] = views[b]

        def weigh(i):
            u, d = units[i]
            if u == 0:
                wide[i] = ring.tile([P, 2, 2 * P], F32, name="wide")
            for b in range(2):
                src = turned[i, b].bitcast(BF16)
                if u == 0:
                    term = wide[i][:, b, :]
                elif i == last - 1 and b == 1:
                    term = held.tile([P, 2 * P], F32, name="term_late", tag="before_w_codes", align_bytes=64)
                else:
                    term = ring.tile([P, 2 * P], F32, name="term", bufs=7)
                dst = term[:]
                src = src.rearrange("v (p e) -> v e p", e=2)
                dst = dst.rearrange("v (e p) -> v e p", e=2)
                g = gate_cols[:, 2 * d + b : 2 * d + b + 1]
                if i in fused:
                    prev = terms[i - 1, b][:].rearrange("v (e p) -> v e p", e=2)
                    nc.vector.scalar_tensor_tensor(dst, src, g, prev, MULT, ADD)
                else:
                    nc.scalar.activation(dst, src, COPY, scale=g)
                terms[i, b] = term

        def add_two(i):
            both = held.tile([P, 2, 2 * P], F32, name="both", tag="before_first_add" if i == 1 else "both")
            nc.gpsimd.tensor_tensor(both[:], wide[i - 1][:], wide[i][:], ADD)
            for b in range(2):
                terms[i, b] = both[:, b, :]

        def add_up(i):
            u = units[i][0]
            for b in range(2):
                for e in range(2):
                    nc.tensor.matmul(
                        sums[b][:, 2 * u + e, :],
                        terms[i, b][:, e * P : (e + 1) * P],
                        ident[:],
                        start=(i == 1 and e == 0),
                        stop=(i == last and e == 1),
                        is_transpose=True,
                    )

        for step in range(len(units) + 1):
            if step <= last:
                pick(step)
            if step >= 1:
                weigh(step - 1)
            if step - 3 in (1, 3):
                add_two(step - 3)
        for i in (1, 4, 3, 7):
            add_up(i)

        w_grouped = held.tile([P, N, PACK], BF16, name="w_grouped", tag="before_w_grouped", align_bytes=64)
        w_codes = held.tile([P, N], U32, name="w_codes", tag="before_w_codes", align_bytes=64)
        halves = [slice(0, P), slice(P, 2 * P)]
        for cols in halves:
            nc.scalar.copy(w_grouped[:, cols, :], w_raw[:, :, cols].rearrange("p t n -> p n t"))

        def quantize(codes, scales, grouped, cols):
            nc.vector.quantize_mx(
                out=codes[:, cols].bitcast(FP8X4),
                scales=scales[:, cols],
                in_=grouped[:, cols, :].rearrange("p c t -> p (c t)"),
            )

        x_codes = held.tile([P, V], U32, name="x_codes", align_bytes=64)
        x_scales = held.tile([P, V], U8, name="x_scales", align_bytes=64)
        quantize(w_codes, w_scales, w_grouped, halves[0])
        nc.vector.tensor_copy(out=x_grouped[:, halves[0], :], in_=sums[0][:].rearrange("p t v -> p v t"))
        nc.scalar.copy(x_grouped[:, halves[1], :], sums[1][:].rearrange("p t v -> p v t"))
        quantize(w_codes, w_scales, w_grouped, halves[1])

        out_rows = out.rearrange("(h m) v -> m h v", h=2)
        for b, bags in enumerate(halves):
            quantize(x_codes, x_scales, x_grouped, bags)
            result = held.tile([P, 2, P], F32, name=f"result{b}")
            for h, cols in enumerate(halves):
                acc = fwd_pool.tile([P, P], F32, name="fwd")
                nc.tensor.matmul_mx(
                    out=acc[:],
                    lhsT=w_codes[:, cols].bitcast(FP8X4),
                    lhsT_scale=w_scales[:, cols],
                    rhs=x_codes[:, bags].bitcast(FP8X4),
                    rhs_scale=x_scales[:, bags],
                    start=True,
                    stop=True,
                )
                if b == 0:
                    nc.scalar.copy(result[:, h, :], acc[:])
                elif h == 0:
                    nc.vector.tensor_copy(out=result[:, h, :], in_=acc[:])
                    nc.sync.dma_start(out=out_rows[:, h, bags], in_=result[:, h, :])
                else:
                    nc.scalar.copy(result[:, h, :], acc[:])
                    nc.scalar.dma_start(out=out_rows[:, h, bags], in_=result[:, h, :])
            if b == 0:
                nc.sync.dma_start(out=out_rows[:, :, bags], in_=result[:])
